import numpy as np
import ml_dtypes


def mxq(x, axis, fmt="e4m3"):
    dtype, down = {"e4m3": (ml_dtypes.float8_e4m3fn, 7), "e5m2": (ml_dtypes.float8_e5m2, 14)}[fmt]
    v = np.moveaxis(np.asarray(x, np.float32).astype(ml_dtypes.bfloat16).astype(np.float64), axis, -1)
    blocks = v.reshape(v.shape[:-1] + (-1, 32))
    amax = np.abs(blocks).max(-1, keepdims=True)
    byte = np.maximum(np.where(amax > 0, np.frexp(amax)[1] - 1 + 127, 0) - down, 1)
    scale = np.exp2(byte - 127.0)
    codes = (blocks / scale).astype(np.float32).astype(dtype).astype(np.float64)
    return np.moveaxis((codes * scale).reshape(v.shape), -1, axis)


WIDE = False


def mx_kscale(k):
    if not WIDE:
        return np.ones(k)
    levels = np.array([10, -10, 5, -5, 0])
    if k % 512:
        return np.exp2(np.random.permutation(np.resize(levels, k // 32))).repeat(32)
    a = np.empty((k // 512, 16))
    for p in range(k // 512):
        a[p, :8] = np.random.permutation(np.resize(levels, 8))
        for g in range(8):
            far = levels[np.abs(levels - a[p, g]) >= 10]
            a[p, g + 8] = far[np.random.randint(len(far))]
    return np.exp2(a.ravel()).repeat(32)


def f64(x):
    return np.asarray(x).astype(np.float64)


def striped(idx):
    return np.tile(np.asarray(idx).reshape(-1, 16).T, (8, 1)).astype(np.uint16)


def unstriped(offs):
    return offs[:16].T.reshape(-1).astype(np.int64)


E2M1 = np.array([0.0, 0.5, 1.0, 1.5, 2.0, 3.0, 4.0, 6.0, -0.0, -0.5, -1.0, -1.5, -2.0, -3.0, -4.0, -6.0])


def pack_weight(w, fmt):
    k, n = w.shape
    w = f64(np.asarray(w, np.float32).astype(ml_dtypes.bfloat16)).reshape(k // 32, 32, n)
    amax = np.abs(w).max(1)
    if fmt == "e4m3":
        byte = np.frexp(amax)[1] - 1 + 127 - 7
    else:
        mant, ex = np.frexp(amax / 6.0)
        byte = np.where(mant > 0.5, ex, ex - 1) + 127
    byte = np.clip(np.where(amax > 0, byte, 1), 1, 254)
    scaled = (w * np.exp2(127.0 - byte)[:, None, :]).reshape(k, n).astype(np.float32)
    by_word = np.ascontiguousarray(scaled.reshape(k // 512, 128, 4, n).transpose(0, 1, 3, 2))
    if fmt == "e4m3":
        words = by_word.astype(ml_dtypes.float8_e4m3fn).view(np.uint8)
    else:
        c = by_word.astype(ml_dtypes.float4_e2m1fn).view(np.uint8) & 0xF
        words = (c[..., 0::2] | (c[..., 1::2] << 4)).reshape(k // 512, 128, 2 * n)
    return np.ascontiguousarray(words), np.ascontiguousarray(byte.astype(np.uint8).reshape(k // 512, 16, n))


def unpack_weight(words, scales, fmt):
    g, _, n = scales.shape
    words = np.ascontiguousarray(words).reshape(g, 128, n, -1)
    if fmt == "e4m3":
        vals = words.view(ml_dtypes.float8_e4m3fn).astype(np.float64)
    else:
        nib = np.empty((g, 128, n, 4), np.uint8)
        nib[..., 0::2] = words & 0xF
        nib[..., 1::2] = words >> 4
        vals = E2M1[nib]
    vals = vals * np.repeat(np.exp2(scales.astype(np.float64) - 127.0), 8, axis=1)[..., None]
    return vals.transpose(0, 1, 3, 2).reshape(g * 512, n)


def sigmoid(v):
    return 1.0 / (1.0 + np.exp(-v))


D, E, T, I, Q = 512, 512, 2048, 512, 128


def setup_inputs():
    n = np.random.standard_normal
    idx = np.random.permutation(T)[:I]
    fd = mx_kscale(D)
    fe = mx_kscale(E)
    keysp = pack_weight(n((D, T)) / fd[:, None], "e2m1")
    valsp = pack_weight(n((E, T)) / fe[:, None], "e2m1")
    return {
        "query": (n((D, Q)) * 0.6 / np.sqrt(D) * fd[:, None]).astype(np.float32),
        "keys_words": keysp[0],
        "keys_scales": keysp[1],
        "th": (np.random.uniform(5.8, 6.8, (Q, 1))).astype(np.float32),
        "steep": (np.random.uniform(1.0, 4.0, (Q, 1))).astype(np.float32),
        "kdot": (np.random.uniform(-1.0, 1.0, (Q, 1))).astype(np.float32),
        "gout": (n((E, Q)) * 1 / np.sqrt(E) * fe[:, None]).astype(np.float32),
        "vals_words": valsp[0],
        "vals_scales": valsp[1],
        "base": (0.5 * n((Q, T))).astype(np.float32),
        "gq1": (np.random.uniform(0.3, 1.5, (Q, 1))).astype(np.float32),
        "offs": striped(idx),
    }


def reference(query, keys_words, keys_scales, th, steep, kdot, gout, vals_words, vals_scales, base, gq1, offs):
    idx = unstriped(offs)
    keysu = unpack_weight(keys_words, keys_scales, "e2m1")
    valsu = unpack_weight(vals_words, vals_scales, "e2m1")
    queryq = mxq(f64(query), 0, "e4m3")
    keysidxg = keysu[:, idx]
    a = queryq.T @ keysidxg
    p = np.exp(a)
    z = np.sum(p, axis=1, keepdims=True)
    gt = sigmoid((np.log(z) - f64(th)) * f64(steep))
    goutq = mxq(f64(gout), 0, "e4m3")
    valsidxg = valsu[:, idx]
    c0 = goutq.T @ valsidxg
    dgt = np.sum(p * c0, axis=1, keepdims=True) / z - f64(kdot)
    dz = dgt * gt * (1.0 - gt) * f64(steep) / z - gt * np.sum(p * c0, axis=1, keepdims=True) / np.square(z)
    dp = gt / z * c0 + dz
    da = dp * p
    hda = da * 512.0 * 2.0 * 512.0
    hdp = hda * p
    hdz = np.sum(hdp, axis=1, keepdims=True)
    hdgt = hdz / z * f64(steep) * (1.0 - gt) * gt
    hgt = np.sum(hdp * c0, axis=1, keepdims=True) / z + hdz / z * f64(steep) * (1.0 - gt) * dgt + hdz * (-1.0) / np.square(z) * np.sum(p * c0, axis=1, keepdims=True) - hdz / z * f64(steep) * dgt * gt
    hz = hdz * (-1.0) * gt * np.sum(p * c0, axis=1, keepdims=True) / np.square(np.square(z)) * (-1.0) * z * 2.0 + hgt * gt * (1.0 - gt) * f64(steep) / z - np.sum(hdp * c0, axis=1, keepdims=True) * gt / np.square(z) - hdz * dgt * gt * (1.0 - gt) * f64(steep) / np.square(z) - hdgt * np.sum(p * c0, axis=1, keepdims=True) / np.square(z)
    hp = hda * dp + hdz * (-1.0) / np.square(z) * gt * c0 + hdgt / z * c0 + hz
    ha = hp * p
    gs = ha * f64(gq1)
    gf = np.zeros((Q, T))
    gf[:, idx] = gs
    y = f64(base) + gf
    return y

from contextlib import ExitStack

import concourse.mybir as mybir

D, E, T, I, Q = 512, 512, 2048, 512, 128
FLOPS = 2 * Q * I * (D + E)

F32 = mybir.dt.float32
BF16 = mybir.dt.bfloat16
I32 = mybir.dt.int32
U32 = mybir.dt.uint32
U16 = mybir.dt.uint16
U8 = mybir.dt.uint8
FP8X4 = mybir.dt.float8_e4m3fn_x4
FP4X4 = mybir.dt.float4_e2m1fn_x4
ALU = mybir.AluOpType
ACT = mybir.ActivationFunctionType
AXIS = mybir.AxisListType

P = 128
PACK = 4
PENALTY = 512.0 * 2.0 * 512.0
CHUNKS = [256, 512, 512, 512, 256]
HALF = I // 2


def load_scales(nc, plane, scales):
    nc.vector.memset(plane[:].bitcast(I32), 0)
    for r in range(4):
        nc.sync.dma_start(out=plane[r:P:32, :].bitcast(I32), in_=scales[0, r:16:4, :].bitcast(I32))


def tile_attend_gpupdategate_kernel(tc, query, keys_words, keys_scales, th, steep, kdot, gout, vals_words,
                                     vals_scales, base, gq1, offs, out):
    nc = tc.nc
    with ExitStack() as ctx:
        held = ctx.enter_context(tc.tile_pool(name="held", bufs=1))
        psum = ctx.enter_context(tc.psum_pool(name="psum", bufs=1))

        def col(name, width=1):
            return held.tile([P, width], F32, name=name)

        def wide(name):
            return held.tile([P, I], F32, name=name, align_bytes=64)

        offsets = held.tile([P, I // 16], U16, name="offsets")
        nc.sync.dma_start(offsets[:], offs)

        warm_in = held.tile([P, 1], F32, name="warm_in", tag="raw")
        warm_out = held.tile([P, 1], F32, name="warm_out", tag="v_words", align_bytes=64)
        nc.vector.memset(warm_in[:], 0.0)
        nc.scalar.activation(out=warm_out[:], in_=warm_in[:], func=ACT.Exp)

        k_words = held.tile([P, T], U16, name="k_words", tag="k_words", align_bytes=64)
        nc.sync.dma_start(out=k_words[:].bitcast(I32), in_=keys_words[0].bitcast(I32))
        k_plane = held.tile([P, T], U8, name="k_plane", tag="k_plane", align_bytes=64)
        load_scales(nc, k_plane, keys_scales)
        raw = held.tile([P, 2, PACK, Q], F32, name="raw", tag="raw")
        nc.sync.dma_start(out=raw[:, 0], in_=query.rearrange("(p j) q -> p j q", j=PACK))
        v_words = held.tile([P, T], U16, name="v_words", tag="v_words", align_bytes=64)
        nc.sync.dma_start(out=v_words[:].bitcast(I32), in_=vals_words[0].bitcast(I32))
        nc.sync.dma_start(out=raw[:, 1], in_=gout.rearrange("(p j) q -> p j q", j=PACK))
        placed = held.tile([P, T], F32, name="placed")
        nc.vector.memset(placed[:].bitcast(I32), 0)
        v_plane = held.tile([P, T], U8, name="v_plane", align_bytes=64)
        load_scales(nc, v_plane, vals_scales)

        def quantise(rows, name):
            grouped = held.tile([P, Q, PACK], BF16, name=name + "_bf", align_bytes=64)
            nc.scalar.copy(out=grouped[:], in_=rows.rearrange("p j q -> p q j"))
            codes = held.tile([P, Q], U32, name=name + "_codes", tag=name + "_codes", align_bytes=64)
            plane = held.tile([P, Q], U8, name=name + "_plane", align_bytes=64)
            nc.vector.quantize_mx(out=codes[:].bitcast(FP8X4), scales=plane[:],
                                  in_=grouped[:].rearrange("p q j -> p (q j)"))
            return codes, plane

        def gather(window, dtype, first, count, name, tag):
            picked = held.tile([P, count], dtype, name=name, tag=tag, align_bytes=64)
            nc.vector.tensor_copy(picked[:], window[:].indirect(offsets[:, first // 16 : (first + count) // 16]))
            return picked

        def product(acc, codes, plane, words, scales):
            nc.tensor.matmul_mx(out=acc, lhsT=codes[:].bitcast(FP8X4), lhsT_scale=plane[:],
                                rhs=words[:].bitcast(FP4X4), rhs_scale=scales[:], start=True, stop=True)

        k_w = gather(k_words, U16, 0, I, "k_w", "k_w")
        params = held.tile([P, 4, 8], F32, name="params", tag="k_words", align_bytes=64)
        th_c, st_c, gq_c, kd_c = (params[:, n, 0:1] for n in range(4))
        for column, src in ((th_c, th), (st_c, steep), (kd_c, kdot), (gq_c, gq1)):
            nc.sync.dma_start(out=column, in_=src)
        k_sc = gather(k_plane, U8, 0, I, "k_sc", "k_sc")
        q_codes, q_plane = quantise(raw[:, 0], "q")
        a = psum.tile([P, I], F32, name="a")
        product(a[:], q_codes, q_plane, k_w, k_sc)
        v_w0 = gather(v_words, U16, 0, HALF, "v_w0", "k_plane")

        neg_m = col("neg_m")
        nc.vector.tensor_reduce(out=neg_m[:], in_=a[:], axis=AXIS.X, op=ALU.max, negate=True)
        g_codes, g_plane = quantise(raw[:, 1], "g")
        c = psum.tile([P, I], F32, name="c")
        v_sc0 = gather(v_plane, U8, 0, HALF, "v_sc0", "k_sc")
        product(c[:, 0:HALF], g_codes, g_plane, v_w0, v_sc0)
        v_w1 = gather(v_words, U16, HALF, HALF, "v_w1", "k_w")
        v_sc1 = gather(v_plane, U8, HALF, HALF, "v_sc1", "q_codes")
        product(c[:, HALF:I], g_codes, g_plane, v_w1, v_sc1)
        base_sb = held.tile([P, T], F32, name="base_sb", tag="v_words", align_bytes=64)
        nc.sync.dma_start(out=base_sb[:], in_=base)

        lines = held.tile([P, 5, 2], F32, name="lines")
        nc.vector.memset(lines[:, 2, 1:2], 0.0)
        nc.vector.memset(lines[:, 4, 1:2], 1.0)
        neg_th, kk, neg_kd = col("neg_th"), col("kk"), col("neg_kd")
        pair = col("pair", 2)
        neg_st = pair[:, 0:1]
        nc.scalar.mul(neg_th[:], th_c, -1.0)
        nc.scalar.mul(neg_st, st_c, -1.0)
        nc.scalar.activation(out=pair[:, 1:2], in_=st_c, func=ACT.Identity, bias=-1.0)
        nc.scalar.mul(lines[:, 3, 0:1], st_c, -1.0)
        nc.scalar.copy(lines[:, 3, 1:2], st_c)
        nc.scalar.copy(lines[:, 4, 0:1], st_c)
        nc.scalar.activation(out=lines[:, 1, 0:1], in_=kd_c, func=ACT.Copy, scale=neg_st)
        nc.scalar.activation(out=lines[:, 1, 1:2], in_=kd_c, func=ACT.Copy, scale=st_c)
        nc.scalar.mul(neg_kd[:], kd_c, -1.0)
        nc.scalar.mul(kk[:], gq_c, PENALTY)

        e, z_sum = wide("e"), col("z_sum")
        shift, ratio, odds, den = col("shift"), col("ratio"), col("odds"), col("den")
        nc.scalar.activation(out=e[:], in_=a[:], func=ACT.Exp, bias=neg_m[:], accum_out=z_sum[:])
        nc.scalar.activation(out=shift[:], in_=neg_m[:], func=ACT.Exp, scale=-1.0, bias=neg_th[:])
        nc.scalar.activation(out=ratio[:], in_=z_sum[:], func=ACT.Copy, scale=shift[:])
        nc.gpsimd.tensor_tensor(out=odds[:], in0=ratio[:], in1=neg_st, op=ALU.pow)
        ee = wide("ee")
        nc.scalar.activation(out=ee[:], in_=e[:], func=ACT.Square)
        nc.scalar.activation(out=den[:], in_=odds[:], func=ACT.Identity, bias=1.0)

        rz = lines[:, 2, 0:1]
        nc.vector.reciprocal(out=rz, in_=z_sum[:])
        nc.vector.tensor_scalar(out=lines[:, 0, :], in0=pair[:], scalar1=rz, scalar2=None, op0=ALU.mult)
        g = col("g")
        nc.vector.reciprocal(out=g[:], in_=den[:])

        u, r_sum = wide("u"), col("r_sum")
        nc.vector.scalar_tensor_tensor(out=u[:], in0=c[:], scalar=1.0, in1=e[:], op0=ALU.mult, op1=ALU.mult,
                                       accum_out=r_sum[:])
        at_g = col("at_g", 5)
        nc.vector.scalar_tensor_tensor(out=at_g[:], in0=lines[:, :, 0], scalar=g[:], in1=lines[:, :, 1],
                                       op0=ALU.mult, op1=ALU.add)
        rho, ksig, grz, sig, sg1 = (at_g[:, n : n + 1] for n in range(5))
        off = col("off")
        nc.vector.tensor_scalar(out=off[:], in0=r_sum[:], scalar1=rho, scalar2=ksig, op0=ALU.mult,
                                op1=ALU.subtract)
        big = col("big")
        nc.vector.tensor_scalar(out=big[:], in0=grz, scalar1=grz, scalar2=kk[:], op0=ALU.mult, op1=ALU.mult)
        x1, u_sum = wide("x1"), col("u_sum")
        nc.vector.scalar_tensor_tensor(out=x1[:], in0=c[:], scalar=off[:], in1=ee[:], op0=ALU.add, op1=ALU.mult,
                                       accum_out=u_sum[:])
        x2, s_sum = wide("x2"), col("s_sum")
        nc.vector.scalar_tensor_tensor(out=x2[:], in0=c[:], scalar=off[:], in1=x1[:], op0=ALU.add, op1=ALU.mult,
                                       accum_out=s_sum[:])

        nphi, nphr, dgt, rkd = col("nphi"), col("nphr"), col("dgt"), col("rkd")
        negf, grho, negfg = col("negf"), col("grho"), col("negfg")
        nc.scalar.activation(out=nphi[:], in_=sg1, func=ACT.Identity, scale=sig, bias=-1.0)
        nc.scalar.activation(out=dgt[:], in_=r_sum[:], func=ACT.Identity, scale=rz, bias=neg_kd[:])
        nc.scalar.activation(out=rkd[:], in_=rho, func=ACT.Copy, scale=kd_c)
        nc.scalar.activation(out=nphr[:], in_=nphi[:], func=ACT.Copy, scale=rz)
        nc.scalar.activation(out=grho[:], in_=big[:], func=ACT.Copy, scale=rho)
        nc.scalar.activation(out=negf[:], in_=dgt[:], func=ACT.Identity, scale=nphr[:], bias=rkd[:])
        nc.scalar.activation(out=negfg[:], in_=negf[:], func=ACT.Copy, scale=big[:])
        q_c, nfu, rb = col("q_c"), col("nfu"), col("rb")
        nc.scalar.activation(out=q_c[:], in_=u_sum[:], func=ACT.Copy, scale=grho[:])
        nc.scalar.activation(out=nfu[:], in_=u_sum[:], func=ACT.Copy, scale=negfg[:])
        qu = wide("qu")
        nc.scalar.activation(out=qu[:], in_=u[:], func=ACT.Copy, scale=q_c[:])
        nc.vector.tensor_scalar(out=rb[:], in0=s_sum[:], scalar1=grho[:], scalar2=nfu[:], op0=ALU.mult,
                                op1=ALU.subtract)
        y1, y2 = wide("y1"), wide("y2")
        nc.vector.scalar_tensor_tensor(out=y1[:], in0=x2[:], scalar=big[:], in1=qu[:], op0=ALU.mult, op1=ALU.add)
        nc.scalar.activation(out=y2[:], in_=e[:], func=ACT.Copy, scale=rb[:])
        nc.vector.tensor_tensor(out=placed[:].indirect(offsets[:]), in0=y1[:], in1=y2[:], op=ALU.add)

        start = 0
        for n, width in enumerate(CHUNKS):
            cols = slice(start, start + width)
            total = held.tile([P, width], F32, name="total%d" % n)
            nc.vector.tensor_tensor(out=total[:], in0=placed[:, cols], in1=base_sb[:, cols], op=ALU.add)
            queue = nc.sync if n % 2 == 0 else nc.scalar
            queue.dma_start(out=out[:, cols], in_=total[:])
            start += width
